import numpy as np
import ml_dtypes


def mxq(x, axis, fmt="e4m3"):
    dtype, down = {"e4m3": (ml_dtypes.float8_e4m3fn, 7), "e5m2": (ml_dtypes.float8_e5m2, 14)}[fmt]
    v = np.moveaxis(np.asarray(x, np.float32).astype(ml_dtypes.bfloat16).astype(np.float64), axis, -1)
    blocks = v.reshape(v.shape[:-1] + (-1, 32))
    amax = np.abs(blocks).max(-1, keepdims=True)
    byte = np.maximum(np.where(amax > 0, np.frexp(amax)[1] - 1 + 127, 0) - down, 1)
    scale = np.exp2(byte - 127.0)
    codes = (blocks / scale).astype(np.float32).astype(dtype).astype(np.float64)
    return np.moveaxis((codes * scale).reshape(v.shape), -1, axis)


WIDE = False


def mx_kscale(k):
    if not WIDE:
        return np.ones(k)
    levels = np.array([10, -10, 5, -5, 0])
    if k % 512:
        return np.exp2(np.random.permutation(np.resize(levels, k // 32))).repeat(32)
    a = np.empty((k // 512, 16))
    for p in range(k // 512):
        a[p, :8] = np.random.permutation(np.resize(levels, 8))
        for g in range(8):
            far = levels[np.abs(levels - a[p, g]) >= 10]
            a[p, g + 8] = far[np.random.randint(len(far))]
    return np.exp2(a.ravel()).repeat(32)


def f64(x):
    return np.asarray(x).astype(np.float64)


def striped(idx):
    return np.tile(np.asarray(idx).reshape(-1, 16).T, (8, 1)).astype(np.uint16)


def unstriped(offs):
    return offs[:16].T.reshape(-1).astype(np.int64)


E2M1 = np.array([0.0, 0.5, 1.0, 1.5, 2.0, 3.0, 4.0, 6.0, -0.0, -0.5, -1.0, -1.5, -2.0, -3.0, -4.0, -6.0])


def pack_weight(w, fmt):
    k, n = w.shape
    w = f64(np.asarray(w, np.float32).astype(ml_dtypes.bfloat16)).reshape(k // 32, 32, n)
    amax = np.abs(w).max(1)
    if fmt == "e4m3":
        byte = np.frexp(amax)[1] - 1 + 127 - 7
    else:
        mant, ex = np.frexp(amax / 6.0)
        byte = np.where(mant > 0.5, ex, ex - 1) + 127
    byte = np.clip(np.where(amax > 0, byte, 1), 1, 254)
    scaled = (w * np.exp2(127.0 - byte)[:, None, :]).reshape(k, n).astype(np.float32)
    by_word = np.ascontiguousarray(scaled.reshape(k // 512, 128, 4, n).transpose(0, 1, 3, 2))
    if fmt == "e4m3":
        words = by_word.astype(ml_dtypes.float8_e4m3fn).view(np.uint8)
    else:
        c = by_word.astype(ml_dtypes.float4_e2m1fn).view(np.uint8) & 0xF
        words = (c[..., 0::2] | (c[..., 1::2] << 4)).reshape(k // 512, 128, 2 * n)
    return np.ascontiguousarray(words), np.ascontiguousarray(byte.astype(np.uint8).reshape(k // 512, 16, n))


def unpack_weight(words, scales, fmt):
    g, _, n = scales.shape
    words = np.ascontiguousarray(words).reshape(g, 128, n, -1)
    if fmt == "e4m3":
        vals = words.view(ml_dtypes.float8_e4m3fn).astype(np.float64)
    else:
        nib = np.empty((g, 128, n, 4), np.uint8)
        nib[..., 0::2] = words & 0xF
        nib[..., 1::2] = words >> 4
        vals = E2M1[nib]
    vals = vals * np.repeat(np.exp2(scales.astype(np.float64) - 127.0), 8, axis=1)[..., None]
    return vals.transpose(0, 1, 3, 2).reshape(g * 512, n)


D, E, T, I, G, U, Q = 512, 512, 4096, 1024, 64, 512, 128


def setup_inputs():
    n = np.random.standard_normal
    idx = np.random.permutation(T)[:I]
    idx2 = np.random.permutation(U)[:G]
    fd = mx_kscale(D)
    fe = mx_kscale(E)
    keysp = pack_weight(n((D, T)) / fd[:, None], "e4m3")
    valsp = pack_weight(n((E, T)) / fe[:, None], "e4m3")
    return {
        "query": (n((D, Q)) * 0.6 / np.sqrt(D) * fd[:, None]).astype(np.float32),
        "keys_words": keysp[0],
        "keys_scales": keysp[1],
        "ptab": (n((Q, U)) * 0.25).astype(np.float32),
        "gout": (n((E, Q)) * 1 / np.sqrt(E) * fe[:, None]).astype(np.float32),
        "vals_words": valsp[0],
        "vals_scales": valsp[1],
        "dquery": (n((D, Q)) * 1.0 / np.sqrt(D) * fd[:, None]).astype(np.float32),
        "base": (0.5 * n((Q, G))).astype(np.float32),
        "offs": striped(idx),
        "offs2": striped(idx2),
    }


def reference(query, keys_words, keys_scales, ptab, gout, vals_words, vals_scales, dquery, base, offs, offs2):
    idx = unstriped(offs)
    idx2 = unstriped(offs2)
    keysu = unpack_weight(keys_words, keys_scales, "e4m3")
    valsu = unpack_weight(vals_words, vals_scales, "e4m3")
    queryq = mxq(f64(query), 0, "e4m3")
    keysidxg = keysu[:, idx]
    a = queryq.T @ keysidxg
    dqueryq = mxq(f64(dquery), 0, "e4m3")
    ta = dqueryq.T @ keysidxg
    x1 = np.exp(a)
    goutq = mxq(f64(gout), 0, "e4m3")
    valsidxg = valsu[:, idx]
    c0 = goutq.T @ valsidxg
    s = x1.reshape(Q, G, I // G).sum(axis=2)
    m1 = (x1 * c0).reshape(Q, G, I // G).sum(axis=2) / s
    tp = np.exp(f64(ptab)[:, idx2])
    p = np.exp(np.log(s) * tp)
    z = np.sum(p, axis=1, keepdims=True)
    dz = np.sum(p * m1, axis=1, keepdims=True) / np.square(z) * (-1.0)
    dp = 1.0 / z * m1 + dz
    xx1 = ta * x1
    xs = xx1.reshape(Q, G, I // G).sum(axis=2)
    xm1 = ((xx1 * c0).reshape(Q, G, I // G).sum(axis=2) - xs * (x1 * c0).reshape(Q, G, I // G).sum(axis=2) / s) / s
    xp = xs / s * tp * p
    xz = np.sum(xp, axis=1, keepdims=True)
    xdz = (np.sum(xp * m1 + xm1 * p, axis=1, keepdims=True) - xz * z * 2.0 * np.sum(p * m1, axis=1, keepdims=True) / np.square(z)) / np.square(z) * (-1.0)
    xdp = xz * 1.0 / np.square(z) * (-1.0) * m1 + xm1 * 1.0 / z + xdz
    xdtp = (xdp * p + xp * dp) * np.log(s) + xs / s * dp * p
    y = xdtp * 8.0 + f64(base)
    return y

@@ -1,0 +1,210 @@
+from contextlib import ExitStack
+
+import concourse.mybir as mybir
+from concourse.masks import make_identity
+
+F32 = mybir.dt.float32
+BF16 = mybir.dt.bfloat16
+I32 = mybir.dt.int32
+U32 = mybir.dt.uint32
+U16 = mybir.dt.uint16
+U8 = mybir.dt.uint8
+FP8X4 = mybir.dt.float8_e4m3fn_x4
+ACT = mybir.ActivationFunctionType
+MULT = mybir.AluOpType.mult
+ADD = mybir.AluOpType.add
+SUB = mybir.AluOpType.subtract
+X = mybir.AxisListType.X
+
+P = 128
+D, T, SLOTS, PAGES, U, Q = 512, 4096, 1024, 64, 512, 128
+PAGE = SLOTS // PAGES
+HALF = SLOTS // 2
+HP = PAGES // 2
+FLOPS = 3 * 2 * D * Q * SLOTS
+LAYOUT = ["pe","pe"]
+VAL_ROW = 4
+CHUNKS = (2, 4)
+
+
+def tile_attend_hvpagepower_kernel(tc, query, keys_words, keys_scales, ptab, gout, vals_words, vals_scales, dquery, base, offs, offs2, out):
+    nc = tc.nc
+    with ExitStack() as ctx:
+        sb = ctx.enter_context(tc.tile_pool(name="sb", bufs=1))
+        ps = ctx.enter_context(tc.psum_pool(name="ps", bufs=1))
+
+        slots = sb.tile([P, SLOTS // 16], U16, name="slots")
+        pages = sb.tile([P, PAGES // 16], U16, name="pages")
+        nc.sync.dma_start(slots[:], offs)
+
+        def load_scales(src, row, name, queue):
+            plane = sb.tile([P, T], U8, name=name, align_bytes=64)
+            nc.vector.memset(plane[:].bitcast(I32), 0)
+            for r in range(4):
+                queue.dma_start(out=plane[row + r : P : 32, :].bitcast(I32), in_=src[0, r:16:4, :].bitcast(I32))
+            return plane
+
+        def load_words(src, name):
+            words = sb.tile([P, T], U32, name=name)
+            nc.sync.dma_start(out=words[:].bitcast(I32), in_=src[0].rearrange("p n t -> p (n t)").bitcast(I32))
+            return words
+
+        def load_rows(src, name):
+            raw = sb.tile([P, 4, Q], F32, name=name)
+            nc.sync.dma_start(out=raw[:], in_=src.rearrange("(p j) w -> p j w", j=4))
+            return raw
+
+        q_raw = load_rows(query, "q_raw")
+        dq_raw = load_rows(dquery, "dq_raw")
+        k_sc = load_scales(keys_scales, 0, "k_sc", nc.sync)
+        v_sc = load_scales(vals_scales, VAL_ROW, "v_sc", nc.gpsimd)
+        k_w = load_words(keys_words, "k_w")
+        ptab_sb = sb.tile([P, U], F32, name="ptab_sb")
+        nc.sync.dma_start(out=ptab_sb[:], in_=ptab)
+        nc.sync.dma_start(pages[:], offs2)
+        g_raw = load_rows(gout, "g_raw")
+        v_w = load_words(vals_words, "v_w")
+        base_sb = sb.tile([P, PAGES], F32, name="base_sb")
+        nc.sync.dma_start(out=base_sb[:], in_=base)
+
+        ident = sb.tile([P, P], F32, name="ident")
+        make_identity(nc, ident[:])
+
+        k_scg = sb.tile([P, SLOTS], U8, name="k_scg", align_bytes=64)
+        nc.vector.tensor_copy(k_scg[:], k_sc[:].indirect(slots[:]))
+
+        qq_bf = sb.tile([P, 2, Q, 4], BF16, name="qq_bf", align_bytes=64)
+        nc.scalar.copy(qq_bf[:, 0], q_raw[:].rearrange("p j w -> p w j"))
+        nc.scalar.copy(qq_bf[:, 1], dq_raw[:].rearrange("p j w -> p w j"))
+        v_scg = sb.tile([P, SLOTS], U8, name="v_scg", tag="k_sc", align_bytes=64)
+        nc.vector.tensor_copy(v_scg[:], v_sc[:].indirect(slots[:]))
+        qq_c = sb.tile([P, 2 * Q], U32, name="qq_c", align_bytes=64)
+        qq_s = sb.tile([P, 2 * Q], U8, name="qq_s", align_bytes=64)
+        nc.vector.quantize_mx(out=qq_c[:].bitcast(FP8X4), scales=qq_s[:], in_=qq_bf[:].rearrange("p a w j -> p (a w j)"))
+
+
+        def gather_words(words, h, name):
+            got = sb.tile([P, HALF], U32, name=name, align_bytes=64)
+            nc.vector.tensor_copy(got[:], words[:].indirect(slots[:, h * 32 : (h + 1) * 32]))
+            return got
+
+        def product(codes, scales, got, got_scales, name):
+            bank = ps.tile([P, HALF], F32, name=name)
+            nc.tensor.matmul_mx(out=bank[:], lhsT=codes.bitcast(FP8X4), lhsT_scale=scales, rhs=got[:].bitcast(FP8X4), rhs_scale=got_scales, start=True, stop=True)
+            return bank
+
+        def by_slot(bank, h):
+            if LAYOUT[h] == "pe":
+                return bank[:].rearrange("p (g j) -> p j g", j=PAGE)
+            return bank[:].rearrange("p (g j) -> p g j", j=PAGE)
+
+        def pair_tile(h, name):
+            shape = [P, PAGE, 2, HP] if LAYOUT[h] == "pe" else [P, 2, HP, PAGE]
+            return sb.tile(shape, F32, name=name)
+
+        def member(tile, h, m):
+            return tile[:, :, m, :] if LAYOUT[h] == "pe" else tile[:, m]
+
+        def turn_and_add(tile, acc_tag, back_tag, name):
+            flat = tile[:].rearrange("p j m g -> p (j m g)")
+            acc = ps.tile([P, P], F32, name=name + "_acc", tag=acc_tag)
+            for c in range(8):
+                nc.tensor.matmul(acc[:], lhsT=flat[:, c * P : (c + 1) * P], rhs=ident[:], is_transpose=True, start=(c == 0), stop=(c == 7))
+            turned = sb.tile([P, P], F32, name=name + "_turned")
+            nc.scalar.copy(turned[:], acc[:])
+            back = ps.tile([P, P], F32, name=name + "_back", tag=back_tag)
+            nc.tensor.transpose(back[:], turned[:], ident[:])
+            return back
+
+        def finish(back, h, dest):
+            nc.vector.tensor_reduce(dest[:, :, h * HP : (h + 1) * HP], back[:].rearrange("p (jj m g) -> p m g jj", jj=2, m=2), X, ADD)
+
+        k_g = [gather_words(k_w, h, "k_g%d" % h) for h in range(2)]
+        a_ps, ta_ps = [], []
+        for h in range(2):
+            cols = slice(h * HALF, (h + 1) * HALF)
+            a_ps.append(product(qq_c[:, 0:Q], qq_s[:, 0:Q], k_g[h], k_scg[:, cols], "a%d" % h))
+            ta_ps.append(product(qq_c[:, Q : 2 * Q], qq_s[:, Q : 2 * Q], k_g[h], k_scg[:, cols], "ta%d" % h))
+
+        xw = [pair_tile(h, "xw%d" % h) for h in range(2)]
+        for h in range(2):
+            nc.scalar.activation(member(xw[h], h, 0), by_slot(a_ps[h], h), ACT.Exp)
+            nc.vector.tensor_tensor(member(xw[h], h, 1), member(xw[h], h, 0), by_slot(ta_ps[h], h), MULT)
+
+        lp = sb.tile([P, PAGES], F32, name="lp")
+        nc.vector.tensor_copy(lp[:], ptab_sb[:].indirect(pages[:]))
+        tp = sb.tile([P, PAGES], F32, name="tp")
+        nc.scalar.activation(tp[:], lp[:], ACT.Exp)
+        warm = sb.tile([P, 1], F32, name="warm")
+        nc.scalar.activation(warm[:], xw[1][:, PAGE - 1, 0, 0:1], ACT.Ln, scale=tp[:, 0:1])
+        sx_back = [turn_and_add(xw[h], ("acc", "a0")[h], ("back", "ta0")[h], "sx%d" % h) for h in range(2)]
+
+        g_bf = sb.tile([P, Q, 4], BF16, name="g_bf", align_bytes=64)
+        nc.scalar.copy(g_bf[:], g_raw[:].rearrange("p j w -> p w j"))
+        g_c = sb.tile([P, Q], U32, name="g_c", align_bytes=64)
+        g_s = sb.tile([P, Q], U8, name="g_s", align_bytes=64)
+        nc.vector.quantize_mx(out=g_c[:].bitcast(FP8X4), scales=g_s[:], in_=g_bf[:].rearrange("p w j -> p (w j)"))
+
+        c_ps = []
+        for h in range(2):
+            got = gather_words(v_w, h, "v_g%d" % h)
+            c_ps.append(product(g_c[:], g_s[:], got, v_scg[VAL_ROW:P, h * HALF : (h + 1) * HALF], "c%d" % h))
+
+        sx = sb.tile([P, 2, PAGES], F32, name="sx", tag="v_g0", align_bytes=64)
+        for h in range(2):
+            finish(sx_back[h], h, sx)
+        coef = sb.tile([P, 4, PAGES], F32, name="coef")
+        y, ln_s, u = coef[:, 0], coef[:, 1], coef[:, 3]
+        nc.scalar.activation(coef[:, 1:3], sx[:, 0:1].to_broadcast([P, 2, PAGES]), ACT.Ln)
+        g1 = sb.tile([P, PAGES], F32, name="g1")
+        nc.vector.tensor_tensor(g1[:], ln_s, tp[:], MULT)
+        r = sb.tile([P, PAGES], F32, name="r")
+        nc.scalar.activation(r[:], ln_s, ACT.Exp, scale=-1.0)
+        p = sb.tile([P, PAGES], F32, name="p")
+        z = sb.tile([P, 1], F32, name="z")
+        nc.scalar.activation(p[:], g1[:], ACT.Exp, accum_out=z[:])
+        r8 = sb.tile([P, PAGES], F32, name="r8")
+        nc.scalar.activation(r8[:], r[:], ACT.Copy, scale=8.0)
+        neg_p = sb.tile([P, 1, PAGES], F32, name="neg_p")
+        nc.scalar.activation(neg_p[:, 0], p[:], ACT.Copy, scale=-1.0)
+        nc.vector.tensor_tensor(u, sx[:, 1], r[:], MULT)
+        zi = sb.tile([P, 1], F32, name="zi")
+        nc.vector.reciprocal(zi[:], z[:])
+        e = sb.tile([P, PAGES], F32, name="e")
+        nc.vector.tensor_tensor(e[:], u, tp[:], MULT)
+        w1 = sb.tile([P, 2, PAGES], F32, name="w1")
+        nc.vector.scalar_tensor_tensor(w1[:, 1], p[:], zi[:], r8[:], MULT, MULT)
+        we = sb.tile([P, PAGES], F32, name="we")
+        rho = sb.tile([P, 1], F32, name="rho")
+        nc.vector.scalar_tensor_tensor(we[:], p[:], zi[:], e[:], MULT, MULT, accum_out=rho[:])
+        h1 = sb.tile([P, PAGES], F32, name="h1")
+        nc.vector.scalar_tensor_tensor(h1[:], e[:], rho[:], u, SUB, SUB)
+        lf = sb.tile([P, PAGES], F32, name="lf")
+        nc.vector.scalar_tensor_tensor(lf[:], e[:], rho[:], ln_s, SUB, MULT)
+        nc.vector.tensor_tensor(w1[:, 0], h1[:], w1[:, 1], MULT)
+        nc.vector.tensor_tensor(y, lf[:], u, ADD)
+        nw = sb.tile([P, 2, PAGES], F32, name="nw")
+        nc.vector.scalar_tensor_tensor(nw[:], coef[:, 0:2], zi[:], neg_p[:].to_broadcast([P, 2, PAGES]), MULT, MULT)
+
+        ab = sb.tile([P, 2, PAGES], F32, name="ab")
+        for h in range(2):
+            prod = pair_tile(h, "prod%d" % h)
+            step = PAGE // CHUNKS[h]
+            for c in range(CHUNKS[h]):
+                js = slice(c * step, (c + 1) * step)
+                nc.vector.tensor_tensor(prod[:, js], xw[h][:, js], by_slot(c_ps[h], h)[:, js].unsqueeze(2).to_broadcast([P, step, 2, HP]), MULT)
+            finish(turn_and_add(prod, ("a1", "acc")[h], ("ta1", "back")[h], "ab%d" % h), h, ab)
+
+        xm = sb.tile([P, 3, PAGES], F32, name="xm")
+        kbar = sb.tile([P, 1], F32, name="kbar")
+        mbar = sb.tile([P, 1], F32, name="mbar")
+        nc.vector.scalar_tensor_tensor(xm[:, 2], ab[:, 0], 1.0, w1[:, 1], MULT, MULT, accum_out=mbar[:])
+        nc.vector.scalar_tensor_tensor(xm[:, 0:2], ab[:], 1.0, w1[:], MULT, MULT, accum_out=kbar[:])
+        terms = sb.tile([P, 4, PAGES], F32, name="terms")
+        part = sb.tile([P, PAGES], F32, name="part")
+        nc.vector.scalar_tensor_tensor(part[:], nw[:, 0], mbar[:], base_sb[:], MULT, ADD)
+        nc.vector.tensor_tensor(terms[:, 0:3], xm[:], coef[:, 1:4], MULT)
+        nc.vector.scalar_tensor_tensor(terms[:, 3], nw[:, 1], kbar[:], part[:], MULT, ADD)
+        res = sb.tile([P, PAGES], F32, name="res")
+        nc.vector.tensor_reduce(res[:], terms[:].rearrange("p k g -> p g k"), X, ADD)
+        nc.sync.dma_start(out=out, in_=res[:])

@@ -22,9 +22,7 @@ PAGE = SLOTS // PAGES
 HALF = SLOTS // 2
 HP = PAGES // 2
 FLOPS = 3 * 2 * D * Q * SLOTS
-LAYOUT = ["pe","pe"]
 VAL_ROW = 4
-CHUNKS = (2, 4)
 
 
 def tile_attend_hvpagepower_kernel(tc, query, keys_words, keys_scales, ptab, gout, vals_words, vals_scales, dquery, base, offs, offs2, out):
@@ -57,7 +55,7 @@ def tile_attend_hvpagepower_kernel(tc, query, keys_words, keys_scales, ptab, gou
         q_raw = load_rows(query, "q_raw")
         dq_raw = load_rows(dquery, "dq_raw")
         k_sc = load_scales(keys_scales, 0, "k_sc", nc.sync)
-        v_sc = load_scales(vals_scales, VAL_ROW, "v_sc", nc.gpsimd)
+        v_sc = load_scales(vals_scales, VAL_ROW, "v_sc", nc.sync)
         k_w = load_words(keys_words, "k_w")
         ptab_sb = sb.tile([P, U], F32, name="ptab_sb")
         nc.sync.dma_start(out=ptab_sb[:], in_=ptab)
@@ -72,16 +70,14 @@ def tile_attend_hvpagepower_kernel(tc, query, keys_words, keys_scales, ptab, gou
 
         k_scg = sb.tile([P, SLOTS], U8, name="k_scg", align_bytes=64)
         nc.vector.tensor_copy(k_scg[:], k_sc[:].indirect(slots[:]))
-
         qq_bf = sb.tile([P, 2, Q, 4], BF16, name="qq_bf", align_bytes=64)
         nc.scalar.copy(qq_bf[:, 0], q_raw[:].rearrange("p j w -> p w j"))
         nc.scalar.copy(qq_bf[:, 1], dq_raw[:].rearrange("p j w -> p w j"))
-        v_scg = sb.tile([P, SLOTS], U8, name="v_scg", tag="k_sc", align_bytes=64)
+        v_scg = sb.tile([P, SLOTS], U8, name="v_scg", align_bytes=64)
         nc.vector.tensor_copy(v_scg[:], v_sc[:].indirect(slots[:]))
         qq_c = sb.tile([P, 2 * Q], U32, name="qq_c", align_bytes=64)
         qq_s = sb.tile([P, 2 * Q], U8, name="qq_s", align_bytes=64)
         nc.vector.quantize_mx(out=qq_c[:].bitcast(FP8X4), scales=qq_s[:], in_=qq_bf[:].rearrange("p a w j -> p (a w j)"))
-
 
         def gather_words(words, h, name):
             got = sb.tile([P, HALF], U32, name=name, align_bytes=64)
@@ -91,33 +87,25 @@ def tile_attend_hvpagepower_kernel(tc, query, keys_words, keys_scales, ptab, gou
         def product(codes, scales, got, got_scales, name):
             bank = ps.tile([P, HALF], F32, name=name)
             nc.tensor.matmul_mx(out=bank[:], lhsT=codes.bitcast(FP8X4), lhsT_scale=scales, rhs=got[:].bitcast(FP8X4), rhs_scale=got_scales, start=True, stop=True)
-            return bank
+            return bank[:].rearrange("p (g i j) -> p i g j", i=PAGE // 2, j=2)
 
-        def by_slot(bank, h):
-            if LAYOUT[h] == "pe":
-                return bank[:].rearrange("p (g j) -> p j g", j=PAGE)
-            return bank[:].rearrange("p (g j) -> p g j", j=PAGE)
+        def pair_tile(name):
+            return sb.tile([P, PAGE // 2, 2, HP, 2], F32, name=name)
 
-        def pair_tile(h, name):
-            shape = [P, PAGE, 2, HP] if LAYOUT[h] == "pe" else [P, 2, HP, PAGE]
-            return sb.tile(shape, F32, name=name)
+        def add_turned(acc, tile):
+            for i in range(PAGE // 2):
+                nc.tensor.matmul(acc, lhsT=tile[:, i].rearrange("p m g j -> p (m g j)"), rhs=ident[:], is_transpose=True, start=(i == 0), stop=(i == PAGE // 2 - 1))
 
-        def member(tile, h, m):
-            return tile[:, :, m, :] if LAYOUT[h] == "pe" else tile[:, m]
-
-        def turn_and_add(tile, acc_tag, back_tag, name):
-            flat = tile[:].rearrange("p j m g -> p (j m g)")
-            acc = ps.tile([P, P], F32, name=name + "_acc", tag=acc_tag)
-            for c in range(8):
-                nc.tensor.matmul(acc[:], lhsT=flat[:, c * P : (c + 1) * P], rhs=ident[:], is_transpose=True, start=(c == 0), stop=(c == 7))
-            turned = sb.tile([P, P], F32, name=name + "_turned")
+        def turn_back(acc, back_tag, name):
+            turned = sb.tile([P, 2, P], F32, name=name + "_turned")
             nc.scalar.copy(turned[:], acc[:])
-            back = ps.tile([P, P], F32, name=name + "_back", tag=back_tag)
-            nc.tensor.transpose(back[:], turned[:], ident[:])
+            back = ps.tile([P, 2, P], F32, name=name + "_back", tag=back_tag)
+            for h in range(2):
+                nc.tensor.transpose(back[:, h], turned[:, h], ident[:])
             return back
 
-        def finish(back, h, dest):
-            nc.vector.tensor_reduce(dest[:, :, h * HP : (h + 1) * HP], back[:].rearrange("p (jj m g) -> p m g jj", jj=2, m=2), X, ADD)
+        def finish(back, dest):
+            nc.vector.tensor_reduce(dest[:].rearrange("p m (h g) -> p h m g", h=2), back[:].rearrange("p h (m g j) -> p h m g j", m=2, j=2), X, ADD)
 
         k_g = [gather_words(k_w, h, "k_g%d" % h) for h in range(2)]
         a_ps, ta_ps = [], []
@@ -126,18 +114,19 @@ def tile_attend_hvpagepower_kernel(tc, query, keys_words, keys_scales, ptab, gou
             a_ps.append(product(qq_c[:, 0:Q], qq_s[:, 0:Q], k_g[h], k_scg[:, cols], "a%d" % h))
             ta_ps.append(product(qq_c[:, Q : 2 * Q], qq_s[:, Q : 2 * Q], k_g[h], k_scg[:, cols], "ta%d" % h))
 
-        xw = [pair_tile(h, "xw%d" % h) for h in range(2)]
+        xw = [pair_tile("xw%d" % h) for h in range(2)]
+        sx_acc = ps.tile([P, 2, P], F32, name="sx_acc")
         for h in range(2):
-            nc.scalar.activation(member(xw[h], h, 0), by_slot(a_ps[h], h), ACT.Exp)
-            nc.vector.tensor_tensor(member(xw[h], h, 1), member(xw[h], h, 0), by_slot(ta_ps[h], h), MULT)
+            nc.scalar.activation(xw[h][:, :, 0], a_ps[h], ACT.Exp)
+            nc.vector.tensor_tensor(xw[h][:, :, 1], xw[h][:, :, 0], ta_ps[h], MULT)
 
         lp = sb.tile([P, PAGES], F32, name="lp")
         nc.vector.tensor_copy(lp[:], ptab_sb[:].indirect(pages[:]))
         tp = sb.tile([P, PAGES], F32, name="tp")
         nc.scalar.activation(tp[:], lp[:], ACT.Exp)
-        warm = sb.tile([P, 1], F32, name="warm")
-        nc.scalar.activation(warm[:], xw[1][:, PAGE - 1, 0, 0:1], ACT.Ln, scale=tp[:, 0:1])
-        sx_back = [turn_and_add(xw[h], ("acc", "a0")[h], ("back", "ta0")[h], "sx%d" % h) for h in range(2)]
+        for h in range(2):
+            add_turned(sx_acc[:, h], xw[h])
+        sx_back = turn_back(sx_acc, "sx_back", "sx")
 
         g_bf = sb.tile([P, Q, 4], BF16, name="g_bf", align_bytes=64)
         nc.scalar.copy(g_bf[:], g_raw[:].rearrange("p j w -> p w j"))
@@ -151,49 +140,60 @@ def tile_attend_hvpagepower_kernel(tc, query, keys_words, keys_scales, ptab, gou
             c_ps.append(product(g_c[:], g_s[:], got, v_scg[VAL_ROW:P, h * HALF : (h + 1) * HALF], "c%d" % h))
 
         sx = sb.tile([P, 2, PAGES], F32, name="sx", tag="v_g0", align_bytes=64)
-        for h in range(2):
-            finish(sx_back[h], h, sx)
-        coef = sb.tile([P, 4, PAGES], F32, name="coef")
-        y, ln_s, u = coef[:, 0], coef[:, 1], coef[:, 3]
-        nc.scalar.activation(coef[:, 1:3], sx[:, 0:1].to_broadcast([P, 2, PAGES]), ACT.Ln)
-        g1 = sb.tile([P, PAGES], F32, name="g1")
-        nc.vector.tensor_tensor(g1[:], ln_s, tp[:], MULT)
-        r = sb.tile([P, PAGES], F32, name="r")
-        nc.scalar.activation(r[:], ln_s, ACT.Exp, scale=-1.0)
+        finish(sx_back, sx)
+        coef = sb.tile([P, 3, PAGES], F32, name="coef")
+        t2, ln_s, y = coef[:, 0], coef[:, 1], coef[:, 2]
+        nc.scalar.activation(ln_s, sx[:, 0], ACT.Ln)
+        g12 = sb.tile([P, 2, PAGES], F32, name="g12")
+        nc.gpsimd.tensor_tensor(g12[:, 0], ln_s, tp[:], MULT)
+        nc.gpsimd.tensor_tensor(g12[:, 1], lp[:], ln_s, SUB)
+        lm1 = sb.tile([P, PAGES], F32, name="lm1")
+        nc.gpsimd.tensor_scalar(lm1[:], ln_s, 1.0, -1.0, MULT, ADD)
+        rr = sb.tile([P, 2, PAGES], F32, name="rr")
         p = sb.tile([P, PAGES], F32, name="p")
         z = sb.tile([P, 1], F32, name="z")
-        nc.scalar.activation(p[:], g1[:], ACT.Exp, accum_out=z[:])
+        nc.scalar.activation(rr[:, 0], ln_s, ACT.Exp, scale=-1.0)
+        nc.scalar.activation(rr[:, 1], g12[:, 1], ACT.Exp)
+        nc.scalar.activation(p[:], g12[:, 0], ACT.Exp, accum_out=z[:])
         r8 = sb.tile([P, PAGES], F32, name="r8")
-        nc.scalar.activation(r8[:], r[:], ACT.Copy, scale=8.0)
+        nc.scalar.activation(r8[:], rr[:, 0], ACT.Copy, scale=8.0)
         neg_p = sb.tile([P, 1, PAGES], F32, name="neg_p")
         nc.scalar.activation(neg_p[:, 0], p[:], ACT.Copy, scale=-1.0)
-        nc.vector.tensor_tensor(u, sx[:, 1], r[:], MULT)
-        zi = sb.tile([P, 1], F32, name="zi")
+        ue = sb.tile([P, 2, PAGES], F32, name="ue")
+        u, e = ue[:, 0], ue[:, 1]
+        nc.gpsimd.tensor_tensor(ue[:], sx[:, 1:2].to_broadcast([P, 2, PAGES]), rr[:], MULT)
+        lu = sb.tile([P, PAGES], F32, name="lu")
+        nc.gpsimd.tensor_tensor(lu[:], lm1[:], u, MULT)
+
+        ab_acc = ps.tile([P, 2, P], F32, name="ab_acc", tag="a0")
+        for h in range(2):
+            prod = pair_tile("prod%d" % h)
+            for rows in (slice(0, 4), slice(4, 8)):
+                for m in range(2):
+                    nc.vector.tensor_tensor(prod[:, rows, m], xw[h][:, rows, m], c_ps[h][:, rows], MULT)
+            add_turned(ab_acc[:, h], prod)
+        ab_back = turn_back(ab_acc, "a1", "ab")
+
+        zi = sb.tile([P, 1], F32, name="zi", tag="xw1")
         nc.vector.reciprocal(zi[:], z[:])
-        e = sb.tile([P, PAGES], F32, name="e")
-        nc.vector.tensor_tensor(e[:], u, tp[:], MULT)
         w1 = sb.tile([P, 2, PAGES], F32, name="w1")
-        nc.vector.scalar_tensor_tensor(w1[:, 1], p[:], zi[:], r8[:], MULT, MULT)
         we = sb.tile([P, PAGES], F32, name="we")
         rho = sb.tile([P, 1], F32, name="rho")
-        nc.vector.scalar_tensor_tensor(we[:], p[:], zi[:], e[:], MULT, MULT, accum_out=rho[:])
-        h1 = sb.tile([P, PAGES], F32, name="h1")
-        nc.vector.scalar_tensor_tensor(h1[:], e[:], rho[:], u, SUB, SUB)
+        nc.vector.scalar_tensor_tensor(we[:], p[:], zi[:], e, MULT, MULT, accum_out=rho[:])
+        nc.vector.scalar_tensor_tensor(w1[:, 1], p[:], zi[:], r8[:], MULT, MULT)
         lf = sb.tile([P, PAGES], F32, name="lf")
-        nc.vector.scalar_tensor_tensor(lf[:], e[:], rho[:], ln_s, SUB, MULT)
-        nc.vector.tensor_tensor(w1[:, 0], h1[:], w1[:, 1], MULT)
+        nc.vector.scalar_tensor_tensor(lf[:], e, rho[:], ln_s, SUB, MULT)
+        h1 = sb.tile([P, PAGES], F32, name="h1")
+        nc.vector.scalar_tensor_tensor(h1[:], e, rho[:], u, SUB, SUB)
         nc.vector.tensor_tensor(y, lf[:], u, ADD)
+        nc.vector.tensor_tensor(t2, lf[:], lu[:], SUB)
+        nc.vector.tensor_tensor(w1[:, 0], h1[:], w1[:, 1], MULT)
         nw = sb.tile([P, 2, PAGES], F32, name="nw")
-        nc.vector.scalar_tensor_tensor(nw[:], coef[:, 0:2], zi[:], neg_p[:].to_broadcast([P, 2, PAGES]), MULT, MULT)
-
+        nc.vector.scalar_tensor_tensor(nw[:], coef[:, 1:3], zi[:], neg_p[:].to_broadcast([P, 2, PAGES]), MULT, MULT)
+        local = sb.tile([P, 2, PAGES], F32, name="local")
+        nc.vector.tensor_tensor(local[:], coef[:, 0:2], w1[:, 1:2].to_broadcast([P, 2, PAGES]), MULT)
         ab = sb.tile([P, 2, PAGES], F32, name="ab")
-        for h in range(2):
-            prod = pair_tile(h, "prod%d" % h)
-            step = PAGE // CHUNKS[h]
-            for c in range(CHUNKS[h]):
-                js = slice(c * step, (c + 1) * step)
-                nc.vector.tensor_tensor(prod[:, js], xw[h][:, js], by_slot(c_ps[h], h)[:, js].unsqueeze(2).to_broadcast([P, step, 2, HP]), MULT)
-            finish(turn_and_add(prod, ("a1", "acc")[h], ("ta1", "back")[h], "ab%d" % h), h, ab)
+        finish(ab_back, ab)
 
         xm = sb.tile([P, 3, PAGES], F32, name="xm")
         kbar = sb.tile([P, 1], F32, name="kbar")
@@ -201,10 +201,9 @@ def tile_attend_hvpagepower_kernel(tc, query, keys_words, keys_scales, ptab, gou
         nc.vector.scalar_tensor_tensor(xm[:, 2], ab[:, 0], 1.0, w1[:, 1], MULT, MULT, accum_out=mbar[:])
         nc.vector.scalar_tensor_tensor(xm[:, 0:2], ab[:], 1.0, w1[:], MULT, MULT, accum_out=kbar[:])
         terms = sb.tile([P, 4, PAGES], F32, name="terms")
-        part = sb.tile([P, PAGES], F32, name="part")
-        nc.vector.scalar_tensor_tensor(part[:], nw[:, 0], mbar[:], base_sb[:], MULT, ADD)
-        nc.vector.tensor_tensor(terms[:, 0:3], xm[:], coef[:, 1:4], MULT)
-        nc.vector.scalar_tensor_tensor(terms[:, 3], nw[:, 1], kbar[:], part[:], MULT, ADD)
+        nc.vector.tensor_tensor(terms[:, 0:2], ab[:], local[:], MULT)
+        nc.vector.scalar_tensor_tensor(terms[:, 2], nw[:, 1], mbar[:], base_sb[:], MULT, ADD)
+        nc.vector.tensor_scalar(terms[:, 3], nw[:, 0], kbar[:], None, MULT)
         res = sb.tile([P, PAGES], F32, name="res")
         nc.vector.tensor_reduce(res[:], terms[:].rearrange("p k g -> p g k"), X, ADD)
         nc.sync.dma_start(out=out, in_=res[:])

from contextlib import ExitStack

import concourse.mybir as mybir
from concourse.masks import make_identity

F32 = mybir.dt.float32
BF16 = mybir.dt.bfloat16
I32 = mybir.dt.int32
U32 = mybir.dt.uint32
U16 = mybir.dt.uint16
U8 = mybir.dt.uint8
FP8X4 = mybir.dt.float8_e4m3fn_x4
ACT = mybir.ActivationFunctionType
MULT = mybir.AluOpType.mult
ADD = mybir.AluOpType.add
SUB = mybir.AluOpType.subtract
X = mybir.AxisListType.X

P = 128
D, T, SLOTS, PAGES, U, Q = 512, 4096, 1024, 64, 512, 128
PAGE = SLOTS // PAGES
HALF = SLOTS // 2
HP = PAGES // 2
FLOPS = 3 * 2 * D * Q * SLOTS
VAL_ROW = 4


def tile_attend_hvpagepower_kernel(tc, query, keys_words, keys_scales, ptab, gout, vals_words, vals_scales, dquery, base, offs, offs2, out):
    nc = tc.nc
    with ExitStack() as ctx:
        sb = ctx.enter_context(tc.tile_pool(name="sb", bufs=1))
        ps = ctx.enter_context(tc.psum_pool(name="ps", bufs=1))

        slots = sb.tile([P, SLOTS // 16], U16, name="slots")
        pages = sb.tile([P, PAGES // 16], U16, name="pages")
        nc.sync.dma_start(slots[:], offs)

        def load_scales(src, row, name, queue):
            plane = sb.tile([P, T], U8, name=name, align_bytes=64)
            nc.vector.memset(plane[:].bitcast(I32), 0)
            for r in range(4):
                queue.dma_start(out=plane[row + r : P : 32, :].bitcast(I32), in_=src[0, r:16:4, :].bitcast(I32))
            return plane

        def load_words(src, name):
            words = sb.tile([P, T], U32, name=name)
            nc.sync.dma_start(out=words[:].bitcast(I32), in_=src[0].rearrange("p n t -> p (n t)").bitcast(I32))
            return words

        def load_rows(src, name):
            raw = sb.tile([P, 4, Q], F32, name=name)
            nc.sync.dma_start(out=raw[:], in_=src.rearrange("(p j) w -> p j w", j=4))
            return raw

        q_raw = load_rows(query, "q_raw")
        dq_raw = load_rows(dquery, "dq_raw")
        k_sc = load_scales(keys_scales, 0, "k_sc", nc.sync)
        v_sc = load_scales(vals_scales, VAL_ROW, "v_sc", nc.sync)
        k_w = load_words(keys_words, "k_w")
        ptab_sb = sb.tile([P, U], F32, name="ptab_sb")
        nc.sync.dma_start(out=ptab_sb[:], in_=ptab)
        nc.sync.dma_start(pages[:], offs2)
        g_raw = load_rows(gout, "g_raw")
        v_w = load_words(vals_words, "v_w")
        base_sb = sb.tile([P, PAGES], F32, name="base_sb")
        nc.sync.dma_start(out=base_sb[:], in_=base)

        ident = sb.tile([P, P], F32, name="ident")
        make_identity(nc, ident[:])

        k_scg = sb.tile([P, SLOTS], U8, name="k_scg", align_bytes=64)
        nc.vector.tensor_copy(k_scg[:], k_sc[:].indirect(slots[:]))
        qq_bf = sb.tile([P, 2, Q, 4], BF16, name="qq_bf", align_bytes=64)
        nc.scalar.copy(qq_bf[:, 0], q_raw[:].rearrange("p j w -> p w j"))
        nc.scalar.copy(qq_bf[:, 1], dq_raw[:].rearrange("p j w -> p w j"))
        v_scg = sb.tile([P, SLOTS], U8, name="v_scg", align_bytes=64)
        nc.vector.tensor_copy(v_scg[:], v_sc[:].indirect(slots[:]))
        qq_c = sb.tile([P, 2 * Q], U32, name="qq_c", align_bytes=64)
        qq_s = sb.tile([P, 2 * Q], U8, name="qq_s", align_bytes=64)
        nc.vector.quantize_mx(out=qq_c[:].bitcast(FP8X4), scales=qq_s[:], in_=qq_bf[:].rearrange("p a w j -> p (a w j)"))

        def gather_words(words, h, name):
            got = sb.tile([P, HALF], U32, name=name, align_bytes=64)
            nc.vector.tensor_copy(got[:], words[:].indirect(slots[:, h * 32 : (h + 1) * 32]))
            return got

        def product(codes, scales, got, got_scales, name):
            bank = ps.tile([P, HALF], F32, name=name)
            nc.tensor.matmul_mx(out=bank[:], lhsT=codes.bitcast(FP8X4), lhsT_scale=scales, rhs=got[:].bitcast(FP8X4), rhs_scale=got_scales, start=True, stop=True)
            return bank[:].rearrange("p (g i j) -> p i g j", i=PAGE // 2, j=2)

        def pair_tile(name):
            return sb.tile([P, PAGE // 2, 2, HP, 2], F32, name=name)

        def add_turned(acc, tile):
            for i in range(PAGE // 2):
                nc.tensor.matmul(acc, lhsT=tile[:, i].rearrange("p m g j -> p (m g j)"), rhs=ident[:], is_transpose=True, start=(i == 0), stop=(i == PAGE // 2 - 1))

        def turn_back(acc, back_tag, name):
            turned = sb.tile([P, 2, P], F32, name=name + "_turned")
            nc.scalar.copy(turned[:], acc[:])
            back = ps.tile([P, 2, P], F32, name=name + "_back", tag=back_tag)
            for h in range(2):
                nc.tensor.transpose(back[:, h], turned[:, h], ident[:])
            return back

        def finish(back, dest):
            nc.vector.tensor_reduce(dest[:].rearrange("p m (h g) -> p h m g", h=2), back[:].rearrange("p h (m g j) -> p h m g j", m=2, j=2), X, ADD)

        k_g = [gather_words(k_w, h, "k_g%d" % h) for h in range(2)]
        a_ps, ta_ps = [], []
        for h in range(2):
            cols = slice(h * HALF, (h + 1) * HALF)
            a_ps.append(product(qq_c[:, 0:Q], qq_s[:, 0:Q], k_g[h], k_scg[:, cols], "a%d" % h))
            ta_ps.append(product(qq_c[:, Q : 2 * Q], qq_s[:, Q : 2 * Q], k_g[h], k_scg[:, cols], "ta%d" % h))

        xw = [pair_tile("xw%d" % h) for h in range(2)]
        sx_acc = ps.tile([P, 2, P], F32, name="sx_acc")
        for h in range(2):
            nc.scalar.activation(xw[h][:, :, 0], a_ps[h], ACT.Exp)
            nc.vector.tensor_tensor(xw[h][:, :, 1], xw[h][:, :, 0], ta_ps[h], MULT)

        lp = sb.tile([P, PAGES], F32, name="lp")
        nc.vector.tensor_copy(lp[:], ptab_sb[:].indirect(pages[:]))
        tp = sb.tile([P, PAGES], F32, name="tp")
        nc.scalar.activation(tp[:], lp[:], ACT.Exp)
        for h in range(2):
            add_turned(sx_acc[:, h], xw[h])
        sx_back = turn_back(sx_acc, "sx_back", "sx")

        g_bf = sb.tile([P, Q, 4], BF16, name="g_bf", align_bytes=64)
        nc.scalar.copy(g_bf[:], g_raw[:].rearrange("p j w -> p w j"))
        g_c = sb.tile([P, Q], U32, name="g_c", align_bytes=64)
        g_s = sb.tile([P, Q], U8, name="g_s", align_bytes=64)
        nc.vector.quantize_mx(out=g_c[:].bitcast(FP8X4), scales=g_s[:], in_=g_bf[:].rearrange("p w j -> p (w j)"))

        c_ps = []
        for h in range(2):
            got = gather_words(v_w, h, "v_g%d" % h)
            c_ps.append(product(g_c[:], g_s[:], got, v_scg[VAL_ROW:P, h * HALF : (h + 1) * HALF], "c%d" % h))

        sx = sb.tile([P, 2, PAGES], F32, name="sx", tag="v_g0", align_bytes=64)
        finish(sx_back, sx)
        coef = sb.tile([P, 3, PAGES], F32, name="coef")
        t2, ln_s, y = coef[:, 0], coef[:, 1], coef[:, 2]
        nc.scalar.activation(ln_s, sx[:, 0], ACT.Ln)
        g12 = sb.tile([P, 2, PAGES], F32, name="g12")
        nc.gpsimd.tensor_tensor(g12[:, 0], ln_s, tp[:], MULT)
        nc.gpsimd.tensor_tensor(g12[:, 1], lp[:], ln_s, SUB)
        lm1 = sb.tile([P, PAGES], F32, name="lm1")
        nc.gpsimd.tensor_scalar(lm1[:], ln_s, 1.0, -1.0, MULT, ADD)
        rr = sb.tile([P, 2, PAGES], F32, name="rr")
        p = sb.tile([P, PAGES], F32, name="p")
        z = sb.tile([P, 1], F32, name="z")
        nc.scalar.activation(rr[:, 0], ln_s, ACT.Exp, scale=-1.0)
        nc.scalar.activation(rr[:, 1], g12[:, 1], ACT.Exp)
        nc.scalar.activation(p[:], g12[:, 0], ACT.Exp, accum_out=z[:])
        r8 = sb.tile([P, PAGES], F32, name="r8")
        nc.scalar.activation(r8[:], rr[:, 0], ACT.Copy, scale=8.0)
        neg_p = sb.tile([P, 1, PAGES], F32, name="neg_p")
        nc.scalar.activation(neg_p[:, 0], p[:], ACT.Copy, scale=-1.0)
        ue = sb.tile([P, 2, PAGES], F32, name="ue")
        u, e = ue[:, 0], ue[:, 1]
        nc.gpsimd.tensor_tensor(ue[:], sx[:, 1:2].to_broadcast([P, 2, PAGES]), rr[:], MULT)
        lu = sb.tile([P, PAGES], F32, name="lu")
        nc.gpsimd.tensor_tensor(lu[:], lm1[:], u, MULT)

        ab_acc = ps.tile([P, 2, P], F32, name="ab_acc", tag="a0")
        for h in range(2):
            prod = pair_tile("prod%d" % h)
            for rows in (slice(0, 4), slice(4, 8)):
                for m in range(2):
                    nc.vector.tensor_tensor(prod[:, rows, m], xw[h][:, rows, m], c_ps[h][:, rows], MULT)
            add_turned(ab_acc[:, h], prod)
        ab_back = turn_back(ab_acc, "a1", "ab")

        zi = sb.tile([P, 1], F32, name="zi", tag="xw1")
        nc.vector.reciprocal(zi[:], z[:])
        w1 = sb.tile([P, 2, PAGES], F32, name="w1")
        we = sb.tile([P, PAGES], F32, name="we")
        rho = sb.tile([P, 1], F32, name="rho")
        nc.vector.scalar_tensor_tensor(we[:], p[:], zi[:], e, MULT, MULT, accum_out=rho[:])
        nc.vector.scalar_tensor_tensor(w1[:, 1], p[:], zi[:], r8[:], MULT, MULT)
        lf = sb.tile([P, PAGES], F32, name="lf")
        nc.vector.scalar_tensor_tensor(lf[:], e, rho[:], ln_s, SUB, MULT)
        h1 = sb.tile([P, PAGES], F32, name="h1")
        nc.vector.scalar_tensor_tensor(h1[:], e, rho[:], u, SUB, SUB)
        nc.vector.tensor_tensor(y, lf[:], u, ADD)
        nc.vector.tensor_tensor(t2, lf[:], lu[:], SUB)
        nc.vector.tensor_tensor(w1[:, 0], h1[:], w1[:, 1], MULT)
        nw = sb.tile([P, 2, PAGES], F32, name="nw")
        nc.vector.scalar_tensor_tensor(nw[:], coef[:, 1:3], zi[:], neg_p[:].to_broadcast([P, 2, PAGES]), MULT, MULT)
        local = sb.tile([P, 2, PAGES], F32, name="local")
        nc.vector.tensor_tensor(local[:], coef[:, 0:2], w1[:, 1:2].to_broadcast([P, 2, PAGES]), MULT)
        ab = sb.tile([P, 2, PAGES], F32, name="ab")
        finish(ab_back, ab)

        xm = sb.tile([P, 3, PAGES], F32, name="xm")
        kbar = sb.tile([P, 1], F32, name="kbar")
        mbar = sb.tile([P, 1], F32, name="mbar")
        nc.vector.scalar_tensor_tensor(xm[:, 2], ab[:, 0], 1.0, w1[:, 1], MULT, MULT, accum_out=mbar[:])
        nc.vector.scalar_tensor_tensor(xm[:, 0:2], ab[:], 1.0, w1[:], MULT, MULT, accum_out=kbar[:])
        terms = sb.tile([P, 4, PAGES], F32, name="terms")
        nc.vector.tensor_tensor(terms[:, 0:2], ab[:], local[:], MULT)
        nc.vector.scalar_tensor_tensor(terms[:, 2], nw[:, 1], mbar[:], base_sb[:], MULT, ADD)
        nc.vector.tensor_scalar(terms[:, 3], nw[:, 0], kbar[:], None, MULT)
        res = sb.tile([P, PAGES], F32, name="res")
        nc.vector.tensor_reduce(res[:], terms[:].rearrange("p k g -> p g k"), X, ADD)
        nc.sync.dma_start(out=out, in_=res[:])
